import numpy as np
import ml_dtypes


def mxq(x, axis, fmt="e4m3"):
    dtype, down = {"e4m3": (ml_dtypes.float8_e4m3fn, 7), "e5m2": (ml_dtypes.float8_e5m2, 14)}[fmt]
    v = np.moveaxis(np.asarray(x, np.float32).astype(ml_dtypes.bfloat16).astype(np.float64), axis, -1)
    blocks = v.reshape(v.shape[:-1] + (-1, 32))
    amax = np.abs(blocks).max(-1, keepdims=True)
    byte = np.maximum(np.where(amax > 0, np.frexp(amax)[1] - 1 + 127, 0) - down, 1)
    scale = np.exp2(byte - 127.0)
    codes = (blocks / scale).astype(np.float32).astype(dtype).astype(np.float64)
    return np.moveaxis((codes * scale).reshape(v.shape), -1, axis)


WIDE = False


def mx_kscale(k):
    if not WIDE:
        return np.ones(k)
    levels = np.array([10, -10, 5, -5, 0])
    if k % 512:
        return np.exp2(np.random.permutation(np.resize(levels, k // 32))).repeat(32)
    a = np.empty((k // 512, 16))
    for p in range(k // 512):
        a[p, :8] = np.random.permutation(np.resize(levels, 8))
        for g in range(8):
            far = levels[np.abs(levels - a[p, g]) >= 10]
            a[p, g + 8] = far[np.random.randint(len(far))]
    return np.exp2(a.ravel()).repeat(32)


def f64(x):
    return np.asarray(x).astype(np.float64)


def striped(idx):
    return np.tile(idx.reshape(-1, 16).T, (8, 1)).astype(np.uint16)


def unstriped(offs):
    return offs[:16].T.reshape(-1).astype(np.int64)


E2M1 = np.array([0.0, 0.5, 1.0, 1.5, 2.0, 3.0, 4.0, 6.0, -0.0, -0.5, -1.0, -1.5, -2.0, -3.0, -4.0, -6.0])


def pack_weight(w, fmt):
    k, n = w.shape
    w = f64(np.asarray(w, np.float32).astype(ml_dtypes.bfloat16)).reshape(k // 32, 32, n)
    amax = np.abs(w).max(1)
    if fmt == "e4m3":
        byte = np.frexp(amax)[1] - 1 + 127 - 7
    else:
        mant, ex = np.frexp(amax / 6.0)
        byte = np.where(mant > 0.5, ex, ex - 1) + 127
    byte = np.clip(np.where(amax > 0, byte, 1), 1, 254)
    scaled = (w * np.exp2(127.0 - byte)[:, None, :]).reshape(k, n).astype(np.float32)
    by_word = np.ascontiguousarray(scaled.reshape(k // 512, 128, 4, n).transpose(0, 1, 3, 2))
    if fmt == "e4m3":
        words = by_word.astype(ml_dtypes.float8_e4m3fn).view(np.uint8)
    else:
        c = by_word.astype(ml_dtypes.float4_e2m1fn).view(np.uint8) & 0xF
        words = (c[..., 0::2] | (c[..., 1::2] << 4)).reshape(k // 512, 128, 2 * n)
    return np.ascontiguousarray(words), np.ascontiguousarray(byte.astype(np.uint8).reshape(k // 512, 16, n))


def unpack_weight(words, scales, fmt):
    g, _, n = scales.shape
    words = np.ascontiguousarray(words).reshape(g, 128, n, -1)
    if fmt == "e4m3":
        vals = words.view(ml_dtypes.float8_e4m3fn).astype(np.float64)
    else:
        nib = np.empty((g, 128, n, 4), np.uint8)
        nib[..., 0::2] = words & 0xF
        nib[..., 1::2] = words >> 4
        vals = E2M1[nib]
    vals = vals * np.repeat(np.exp2(scales.astype(np.float64) - 127.0), 8, axis=1)[..., None]
    return vals.transpose(0, 1, 3, 2).reshape(g * 512, n)


def gelu(v):
    return 0.5 * v * (1.0 + np.tanh(np.sqrt(2.0 / np.pi) * (v + 0.044715 * v**3)))


def striped8(idx):
    return np.concatenate([v.reshape(-1, 16).T for v in idx]).astype(np.uint16)


def unstriped8(offs):
    return np.stack([offs[16 * g:16 * g + 16].T.reshape(-1) for g in range(8)]).astype(np.int64)


def heads(h, wgt, idx8):
    r = np.arange(h.shape[0])
    return wgt[r // 4 % 128] * h[r[:, None], idx8[r % 512 // 64]]


def put_heads(h, wgs, idx8, t2):
    r = np.arange(h.shape[0])
    page = np.zeros((h.shape[0], t2))
    page[r[:, None], idx8[r % 512 // 64]] = wgs[r // 4 % 128] * h
    return page


T, S, P, T2, K, H, N = 4096, 1024, 512, 1024, 1024, 1024, 512

def setup_inputs():
    n = np.random.standard_normal
    s = mx_kscale(K)[:, None]
    u = mx_kscale(H)[:, None]
    d = {}
    d["tab_words"], d["tab_scales"] = pack_weight(n((K, T)) * s, "e4m3")
    d["offs"] = striped(np.random.permutation(T)[:S])
    d["offs2"] = striped8(np.stack([np.random.permutation(S)[:P] for _ in range(8)]))
    d["offs3"] = striped8(np.stack([np.random.permutation(T2)[:P] for _ in range(8)]))
    d["w1"] = (1.2 * n((K, H)) / s / K**0.5).astype(np.float32)
    d["w2_words"], d["w2_scales"] = pack_weight(1.5 * n((K, H)) / s / K**0.5, "e2m1")
    d["w3"] = (1.4 * n((H, N)) / u / H**0.5).astype(np.float32)
    d["gain"] = (u[:, 0] * np.exp(0.3 * n(H))).astype(np.float32)
    d["wgt"] = np.repeat(np.random.uniform(0.5, 2.0, (8, P)), 16, axis=0).astype(np.float32)
    d["wgo"] = np.repeat(np.random.uniform(0.5, 2.0, (8, P)), 16, axis=0).astype(np.float32)
    return d

def reference(tab_words, tab_scales, offs, offs2, offs3, w1, w2_words, w2_scales, w3, gain, wgt, wgo):
    v = unpack_weight(tab_words, tab_scales, "e4m3")[:, unstriped(offs)]
    a = mxq(f64(w1), 0, "e4m3").T @ v
    b = unpack_weight(w2_words, w2_scales, "e2m1").T @ v
    h = (b + np.square(a)) / (1.0 + np.abs(a))
    x = heads(h, f64(wgt), unstriped8(offs2))
    z = np.tanh(x) * f64(gain)[:, None]
    y = mxq(f64(w3), 0, "e4m3").T @ mxq(z, 0, "e4m3")
    out = put_heads(y, f64(wgo), unstriped8(offs3), T2)
    return out

@@ -1,0 +1,301 @@
+from contextlib import ExitStack
+
+import concourse.mybir as mybir
+
+F32 = mybir.dt.float32
+BF16 = mybir.dt.bfloat16
+I32 = mybir.dt.int32
+U32 = mybir.dt.uint32
+U16 = mybir.dt.uint16
+U8 = mybir.dt.uint8
+FP8X4 = mybir.dt.float8_e4m3fn_x4
+FP4X4 = mybir.dt.float4_e2m1fn_x4
+ACT = mybir.ActivationFunctionType
+ADD = mybir.AluOpType.add
+MULT = mybir.AluOpType.mult
+
+T, S, M, T2, K, H, N = 4096, 1024, 512, 1024, 1024, 1024, 512
+FLOPS = 2 * (2 * K * H * S + H * N * M)
+
+P = 128
+PACK = 4
+PASS = P * PACK
+BANK = 512
+HALF = M // 2
+LN_FLOOR = 2.0**-60
+RAW_AT = (0, 8192)
+W2_AT = 16384
+TAB_AT = (20480, 36864)
+
+
+def tile_list_muon_void_scores_kernel(
+    tc, tab_words, tab_scales, offs, offs2, offs3, w1, w2_words, w2_scales, w3, gain, wgt, wgo, out
+):
+    nc = tc.nc
+    with ExitStack() as ctx:
+        lists = ctx.enter_context(tc.tile_pool(name="lists", bufs=1))
+        keep = ctx.enter_context(tc.tile_pool(name="keep", bufs=1))
+        ring = ctx.enter_context(tc.tile_pool(name="ring", bufs=1))
+        placed = ctx.enter_context(tc.tile_pool(name="placed", bufs=1))
+        psum = ctx.enter_context(tc.psum_pool(name="psum", bufs=4))
+
+        def held(name, shape, dtype):
+            return keep.tile(shape, dtype, name=name, align_bytes=64)
+
+        idx1 = lists.tile([P, S // 16], U16, name="idx1")
+        idx2 = lists.tile([P, M // 16], U16, name="idx2")
+        idx3 = lists.tile([P, M // 16], U16, name="idx3")
+
+        tab_sc = held("tab_sc", [P, 2, T], U8)
+        w2_sc_raw = ring.tile([P, 2, H], U8, name="w2_sc_raw", tag="w2_sc_raw", bufs=1, align_bytes=64)
+        v_planes = [held(f"v_sc{a}", [P, S], U8) for a in range(2)]
+        act_const = held("act_const", [P, 1], F32)
+        neg_half = held("neg_half", [P, 1], F32)
+        warm_in = placed.tile([P, 16], F32, name="warm_in", offset=W2_AT - 32)
+        warm_out = placed.tile([P, 16], F32, name="warm_out", offset=TAB_AT[1] - 32)
+        pages = [held(f"page{i}", [P, T2], F32) for i in range(PACK)]
+
+        nc.vector.memset(tab_sc[:].rearrange("p a t -> p (a t)").bitcast(I32), 0)
+        nc.vector.memset(warm_in[:], 1.0)
+        nc.vector.memset(act_const[:], LN_FLOOR)
+        nc.vector.memset(neg_half[:], -0.5)
+        nc.vector.memset(w2_sc_raw[:].rearrange("p a c -> p (a c)").bitcast(I32), 0)
+        nc.scalar.activation(warm_out[:], warm_in[:], ACT.Ln)
+        for page in pages:
+            nc.vector.memset(page[:], 0.0)
+
+        def load_weight(name, w, rows, cols):
+            raw = placed.tile([P, PACK, BANK], F32, name=name, offset=RAW_AT[rows])
+            nc.sync.dma_start(
+                out=raw[:],
+                in_=w[PASS * rows : PASS * (rows + 1), BANK * cols : BANK * (cols + 1)].rearrange(
+                    "(p j) c -> p j c", j=PACK
+                ),
+            )
+            return raw
+
+        def deal_weight(raw, copy):
+            grouped = ring.tile([P, PACK * BANK], BF16, name="w_bf", tag="w_bf", bufs=3, align_bytes=64)
+            copy(
+                grouped[:].rearrange("p (t m j) -> p m j t", t=PACK, j=PACK),
+                raw[:].rearrange("p j (m t) -> p m j t", t=PACK),
+            )
+            return grouped
+
+        def quantise(name, grouped):
+            width = grouped.shape[1] // PACK
+            codes = held(name + "_codes", [P, width], U32)
+            scales = held(name + "_scales", [P, width], U8)
+            nc.vector.quantize_mx(out=codes[:].bitcast(FP8X4), scales=scales[:], in_=grouped[:])
+            return codes, scales
+
+        nc.sync.dma_start(idx1[:], offs)
+        nc.sync.dma_start(idx2[:], offs2)
+        nc.sync.dma_start(idx3[:], offs3)
+        w1_raw = {(0, 0): load_weight("w1_raw00", w1, 0, 0)}
+        for q in range(4):
+            nc.sync.dma_start(
+                out=tab_sc[32 * q : 32 * q + 4, :, :].bitcast(I32),
+                in_=tab_scales[:, 4 * q : 4 * q + 4, :].rearrange("a r t -> r a t").bitcast(I32),
+            )
+        w1_raw[1, 0] = load_weight("w1_raw10", w1, 1, 0)
+        for q in range(4):
+            nc.sync.dma_start(
+                out=w2_sc_raw[32 * q : 32 * q + 4, :, :].bitcast(I32),
+                in_=w2_scales[:, 4 * q : 4 * q + 4, :].rearrange("a r c -> r a c").bitcast(I32),
+            )
+        w2_raw = placed.tile([P, 2, 2 * H], U8, name="w2_raw", offset=W2_AT)
+        nc.sync.dma_start(out=w2_raw[:].bitcast(I32), in_=w2_words.rearrange("a p c -> p a c").bitcast(I32))
+        tabs = []
+        for a in range(2):
+            tab = placed.tile([P, T], U32, name=f"tab{a}", offset=TAB_AT[a])
+            nc.sync.dma_start(
+                out=tab[:].bitcast(I32), in_=tab_words[a].rearrange("p t i -> p (t i)").bitcast(I32)
+            )
+            tabs.append(tab)
+        for a in range(2):
+            nc.vector.tensor_copy(v_planes[a][:], tab_sc[:, a, :].indirect(idx1[:]))
+
+        w1_q = {}
+        w1_bf = [deal_weight(w1_raw[a, 0], nc.scalar.copy) for a in range(2)]
+
+        w2_codes = held("w2_codes", [P, 2, 2 * H], U8)
+        w2_sc = held("w2_sc", [P, 2, H], U8)
+        nc.vector.tensor_copy(
+            w2_codes[:].bitcast(U16).rearrange("p a (b t m) -> p (a b) m t", b=2, t=PACK),
+            w2_raw[:].bitcast(U16).rearrange("p a (b m t) -> p (a b) m t", b=2, t=PACK),
+        )
+        nc.vector.tensor_copy(
+            w2_sc[:].rearrange("p a (b t m) -> p (a b) m t", b=2, t=PACK),
+            w2_sc_raw[:].rearrange("p a (b m t) -> p (a b) m t", b=2, t=PACK),
+        )
+        for a in range(2):
+            w1_raw[a, 1] = load_weight(f"w1_raw{a}1", w1, a, 1)
+        weights = placed.tile([P, 2, M], F32, name="weights", offset=W2_AT)
+        wgt_sb, wgo_sb = weights[:, 0, :], weights[:, 1, :]
+        gain_sb = ring.tile([P, 2, PACK], F32, name="gain_sb", tag="w2_sc_raw", bufs=1, align_bytes=64)
+        nc.sync.dma_start(out=wgt_sb, in_=wgt)
+        nc.sync.dma_start(out=gain_sb[:], in_=gain.rearrange("(b p i) -> p b i", b=2, i=PACK))
+        nc.sync.dma_start(out=wgo_sb, in_=wgo)
+        w3_raw = {}
+        for a in range(2):
+            w1_q[a, 0] = quantise(f"w1_{a}0", w1_bf[a])
+
+        v_words = {}
+
+        def gather_words(a, u):
+            words = held(f"v_words{a}{u}", [P, BANK], U32)
+            cols = BANK // 16
+            nc.vector.tensor_copy(words[:], tabs[a][:].indirect(idx1[:, cols * u : cols * (u + 1)]))
+            v_words[a, u] = words
+
+        for a in range(2):
+            for u in range(2):
+                gather_words(a, u)
+
+        def product_a(acc, a, b, t, u):
+            codes, scales = w1_q[a, b]
+            cols = slice(P * t, P * (t + 1))
+            nc.tensor.matmul_mx(
+                out=acc[:],
+                lhsT=codes[:, cols].bitcast(FP8X4),
+                lhsT_scale=scales[:, cols],
+                rhs=v_words[a, u][:].bitcast(FP8X4),
+                rhs_scale=v_planes[a][:, BANK * u : BANK * (u + 1)],
+                start=(a == 0),
+                stop=(a == 1),
+            )
+
+        def product_b(acc, a, b, t, u):
+            first = BANK * b + P * t
+            nc.tensor.matmul_mx(
+                out=acc[:],
+                lhsT=w2_codes[:, a, 2 * first : 2 * (first + P)].bitcast(FP4X4),
+                lhsT_scale=w2_sc[:, a, first : first + P],
+                rhs=v_words[a, u][:].bitcast(FP8X4),
+                rhs_scale=v_planes[a][:, BANK * u : BANK * (u + 1)],
+                start=(a == 0),
+                stop=(a == 1),
+            )
+
+        logs = [held(f"log{s}", [P, S], F32) for s in range(2 * PACK)]
+        rows = [held(f"row{s}", [P, S], F32) for s in range(2 * PACK)]
+
+        def leave_psum(acc_a, acc_b, b, t, u):
+            s = PACK * b + t
+            cols = slice(BANK * u, BANK * (u + 1))
+            sq = ring.tile([P, BANK], F32, name="sq", tag="sq", bufs=4)
+            nc.scalar.activation(sq[:], acc_a[:], ACT.Square)
+            nc.vector.tensor_tensor(rows[s][:, cols], acc_b[:], sq[:], ADD)
+            nc.scalar.activation(logs[s][:, cols], sq[:], ACT.Ln, bias=act_const[:])
+
+        w3_q = {}
+        for b in range(2):
+            for u in range(2):
+                accs = [
+                    (psum.tile([P, BANK], F32, name="acc_a", tag="acc_a"), psum.tile([P, BANK], F32, name="acc_b", tag="acc_b"))
+                    for t in range(PACK)
+                ]
+                first_group = b == 0 and u == 0
+                if first_group:
+                    for t in range(PACK):
+                        product_a(accs[t][0], 0, b, t, u)
+                        product_b(accs[t][1], 0, b, t, u)
+                for t in range(PACK):
+                    for product, acc in zip((product_a, product_b), accs[t]):
+                        for a in range(1 if first_group else 0, 2):
+                            product(acc, a, b, t, u)
+                    leave_psum(accs[t][0], accs[t][1], b, t, u)
+                    if b == 0 and u == 0 and t in (1, 3):
+                        a = t // 2
+                        w1_bf[a] = deal_weight(w1_raw[a, 1], nc.vector.tensor_copy)
+                        w3_raw[a] = load_weight(f"w3_raw{a}", w3, a, 0)
+                    if b == 0 and (u, t) in ((0, 2), (1, 0)):
+                        a = u
+                        w1_q[a, 1] = quantise(f"w1_{a}1", w1_bf[a])
+                    if b == 1 and t == 0:
+                        w1_bf[u] = deal_weight(w3_raw[u], nc.vector.tensor_copy)
+                    if b == 1 and t == 1:
+                        w3_q[u] = quantise(f"w3_{u}", w1_bf[u])
+
+        nc.scalar.copy(act_const[:], neg_half[:])
+        picked = [
+            placed.tile([P, 2, PACK, HALF], F32, name=f"picked{b}", offset=TAB_AT[b]) for b in range(2)
+        ]
+
+        def finish_row(s):
+            nc.scalar.activation(logs[s][:], logs[s][:], ACT.Sigmoid, scale=act_const[:])
+            nc.vector.tensor_tensor(rows[s][:], rows[s][:], logs[s][:], MULT)
+
+        def pick(s, half):
+            b, i = divmod(s, PACK)
+            cols = HALF // 16
+            x = picked[b][:, half, i, :]
+            nc.vector.tensor_tensor(
+                x,
+                rows[s][:].indirect(idx2[:, cols * half : cols * (half + 1)]),
+                wgt_sb[:, HALF * half : HALF * (half + 1)],
+                MULT,
+            )
+            nc.scalar.activation(x, x, ACT.Tanh)
+            nc.scalar.activation(x, x, ACT.Copy, scale=gain_sb[:, b, i : i + 1])
+
+        def weave(b, half):
+            z_bf = ring.tile([P, PACK * HALF], BF16, name="z_bf", tag="z_bf", bufs=2, align_bytes=64)
+            nc.scalar.copy(
+                z_bf[:].rearrange("p (c n i) -> p c i n", n=4, i=PACK),
+                picked[b][:, half, :, :].rearrange("p i (c n) -> p c i n", n=4),
+            )
+            return z_bf
+
+        def product_y(accs, b, z_q):
+            codes, scales = w3_q[b]
+            for i in range(PACK):
+                cols = slice(P * i, P * (i + 1))
+                nc.tensor.matmul_mx(
+                    out=accs[i][:],
+                    lhsT=codes[:, cols].bitcast(FP8X4),
+                    lhsT_scale=scales[:, cols],
+                    rhs=z_q[0][:].bitcast(FP8X4),
+                    rhs_scale=z_q[1][:],
+                    start=(b == 0),
+                    stop=(b == 1),
+                )
+
+        def place(accs, half):
+            cols = HALF // 16
+            for i in range(PACK):
+                y = ring.tile([P, HALF], F32, name="y", tag="y", bufs=4)
+                nc.scalar.copy(y[:], accs[i][:])
+                nc.vector.tensor_tensor(
+                    pages[i][:].indirect(idx3[:, cols * half : cols * (half + 1)]),
+                    y[:],
+                    wgo_sb[:, HALF * half : HALF * (half + 1)],
+                    MULT,
+                )
+                if half == 1:
+                    nc.sync.dma_start(out=out.rearrange("(p i) c -> i p c", i=PACK)[i], in_=pages[i][:])
+
+        y_accs = [
+            [psum.tile([P, HALF], F32, name="acc_y", tag=tag) for i in range(PACK)] for tag in ("acc_a", "acc_b")
+        ]
+        z_bf = {}
+        finish_row(0)
+        for s in range(2 * PACK):
+            if s + 1 < 2 * PACK:
+                finish_row(s + 1)
+            pick(s, 0)
+            if s % PACK == PACK - 1:
+                z_bf[s // PACK, 0] = weave(s // PACK, 0)
+            if s == PACK + 1:
+                product_y(y_accs[0], 0, quantise("z00", z_bf[0, 0]))
+        for s in range(2 * PACK):
+            pick(s, 1)
+            if s % PACK == PACK - 1:
+                z_bf[s // PACK, 1] = weave(s // PACK, 1)
+            if s == PACK:
+                product_y(y_accs[0], 1, quantise("z10", z_bf[1, 0]))
+        product_y(y_accs[1], 0, quantise("z01", z_bf[0, 1]))
+        place(y_accs[0], 0)
+        product_y(y_accs[1], 1, quantise("z11", z_bf[1, 1]))
+        place(y_accs[1], 1)

@@ -21,11 +21,22 @@ P = 128
 PACK = 4
 PASS = P * PACK
 BANK = 512
+QUADRANTS = 4
+PER_COLUMN = 16
+ROW_TILES = H // P
 HALF = M // 2
+IN_PSUM = 4
 LN_FLOOR = 2.0**-60
-RAW_AT = (0, 8192)
-W2_AT = 16384
-TAB_AT = (20480, 36864)
+
+RAW_BYTES = PACK * BANK * 4
+RAW_AT = (0, RAW_BYTES)
+W2_AT = 2 * RAW_BYTES
+TAB_AT = (W2_AT + 2 * H, W2_AT + 2 * H + 4 * T)
+TAB_SC_AT = TAB_AT[1] + 4 * T
+PICKS_AT = TAB_AT[0]
+WEIGHTS_AT = PICKS_AT + ROW_TILES * HALF * 4
+GAIN_AT = WEIGHTS_AT + 2 * M * 4
+W3_AT = TAB_AT[1]
 
 
 def tile_list_muon_void_scores_kernel(
@@ -37,265 +48,319 @@ def tile_list_muon_void_scores_kernel(
         keep = ctx.enter_context(tc.tile_pool(name="keep", bufs=1))
         ring = ctx.enter_context(tc.tile_pool(name="ring", bufs=1))
         placed = ctx.enter_context(tc.tile_pool(name="placed", bufs=1))
-        psum = ctx.enter_context(tc.psum_pool(name="psum", bufs=4))
+        psum = ctx.enter_context(tc.psum_pool(name="psum", bufs=IN_PSUM))
 
         def held(name, shape, dtype):
             return keep.tile(shape, dtype, name=name, align_bytes=64)
 
-        idx1 = lists.tile([P, S // 16], U16, name="idx1")
-        idx2 = lists.tile([P, M // 16], U16, name="idx2")
-        idx3 = lists.tile([P, M // 16], U16, name="idx3")
+        def entries(idx, first, count):
+            return idx[:, first // PER_COLUMN : (first + count) // PER_COLUMN]
 
-        tab_sc = held("tab_sc", [P, 2, T], U8)
-        w2_sc_raw = ring.tile([P, 2, H], U8, name="w2_sc_raw", tag="w2_sc_raw", bufs=1, align_bytes=64)
-        v_planes = [held(f"v_sc{a}", [P, S], U8) for a in range(2)]
+        idx1 = lists.tile([P, S // PER_COLUMN], U16, name="idx1")
+        idx2 = lists.tile([P, M // PER_COLUMN], U16, name="idx2")
+        idx3 = lists.tile([P, M // PER_COLUMN], U16, name="idx3")
+
+        tab_sc = placed.tile([P, T], U8, name="tab_sc", offset=TAB_SC_AT)
+        w2_sc_raw = held("w2_sc_raw", [P, 2, H], U8)
+        v_planes = [held(f"v_plane{g}", [P, S], U8) for g in range(2)]
         act_const = held("act_const", [P, 1], F32)
         neg_half = held("neg_half", [P, 1], F32)
-        warm_in = placed.tile([P, 16], F32, name="warm_in", offset=W2_AT - 32)
-        warm_out = placed.tile([P, 16], F32, name="warm_out", offset=TAB_AT[1] - 32)
+        warm = held("warm", [P, 1], F32)
         pages = [held(f"page{i}", [P, T2], F32) for i in range(PACK)]
 
-        nc.vector.memset(tab_sc[:].rearrange("p a t -> p (a t)").bitcast(I32), 0)
-        nc.vector.memset(warm_in[:], 1.0)
+        nc.vector.memset(tab_sc[:].bitcast(I32), 0)
         nc.vector.memset(act_const[:], LN_FLOOR)
         nc.vector.memset(neg_half[:], -0.5)
-        nc.vector.memset(w2_sc_raw[:].rearrange("p a c -> p (a c)").bitcast(I32), 0)
-        nc.scalar.activation(warm_out[:], warm_in[:], ACT.Ln)
+        nc.vector.memset(w2_sc_raw[:].rearrange("p g c -> p (g c)").bitcast(I32), 0)
+        nc.vector.memset(v_planes[1][:].bitcast(I32), 0)
+        nc.scalar.activation(warm[:], act_const[:], ACT.Ln)
         for page in pages:
             nc.vector.memset(page[:], 0.0)
 
-        def load_weight(name, w, rows, cols):
-            raw = placed.tile([P, PACK, BANK], F32, name=name, offset=RAW_AT[rows])
+        def load_weight(name, w, g, first_column, at):
+            raw = placed.tile([P, PACK, BANK], F32, name=name, offset=at)
             nc.sync.dma_start(
                 out=raw[:],
-                in_=w[PASS * rows : PASS * (rows + 1), BANK * cols : BANK * (cols + 1)].rearrange(
+                in_=w[PASS * g : PASS * (g + 1), first_column : first_column + BANK].rearrange(
                     "(p j) c -> p j c", j=PACK
                 ),
             )
             return raw
 
-        def deal_weight(raw, copy):
-            grouped = ring.tile([P, PACK * BANK], BF16, name="w_bf", tag="w_bf", bufs=3, align_bytes=64)
-            copy(
-                grouped[:].rearrange("p (t m j) -> p m j t", t=PACK, j=PACK),
-                raw[:].rearrange("p j (m t) -> p m j t", t=PACK),
+        def load_w2(b):
+            raw = placed.tile([P, 2, 2 * BANK], U8, name=f"w2_raw{b}", offset=W2_AT)
+            nc.sync.dma_start(
+                out=raw[:].bitcast(I32),
+                in_=w2_words[:, :, 2 * BANK * b : 2 * BANK * (b + 1)].rearrange("g p c -> p g c").bitcast(I32),
             )
-            return grouped
+            return raw
 
-        def quantise(name, grouped):
-            width = grouped.shape[1] // PACK
-            codes = held(name + "_codes", [P, width], U32)
-            scales = held(name + "_scales", [P, width], U8)
-            nc.vector.quantize_mx(out=codes[:].bitcast(FP8X4), scales=scales[:], in_=grouped[:])
+        def load_table(g):
+            tab = placed.tile([P, T], U32, name=f"tab{g}", offset=TAB_AT[g])
+            nc.sync.dma_start(out=tab[:].bitcast(I32), in_=tab_words[g].rearrange("p t i -> p (t i)").bitcast(I32))
+            return tab
+
+        def staging():
+            staged = ring.tile([P, PACK * BANK], BF16, name="w_bf", tag="w_bf", bufs=2, align_bytes=64)
+            return staged[:]
+
+        def deal_weight(raw, copy, staged):
+            copy(
+                staged.rearrange("p (i m j) -> p m j i", i=PACK, j=PACK),
+                raw[:].rearrange("p j (m i) -> p m j i", i=PACK),
+            )
+            return staged
+
+        def quantise(name, staged, codes):
+            scales = held(name + "_scales", [P, codes.shape[1]], U8)
+            nc.vector.quantize_mx(out=codes[:].bitcast(FP8X4), scales=scales[:], in_=staged)
             return codes, scales
+
+        def quantise_held(name, staged):
+            return quantise(name, staged, held(name + "_codes", [P, staged.shape[1] // PACK], U32))
 
         nc.sync.dma_start(idx1[:], offs)
         nc.sync.dma_start(idx2[:], offs2)
         nc.sync.dma_start(idx3[:], offs3)
-        w1_raw = {(0, 0): load_weight("w1_raw00", w1, 0, 0)}
-        for q in range(4):
+        w1_raw = {(0, 0): load_weight("w1_raw00", w1, 0, 0, RAW_AT[0])}
+        for q in range(QUADRANTS):
             nc.sync.dma_start(
-                out=tab_sc[32 * q : 32 * q + 4, :, :].bitcast(I32),
-                in_=tab_scales[:, 4 * q : 4 * q + 4, :].rearrange("a r t -> r a t").bitcast(I32),
+                out=tab_sc[32 * q : 32 * q + 8, :].bitcast(I32),
+                in_=tab_scales[:, 4 * q : 4 * q + 4, :].bitcast(I32),
             )
-        w1_raw[1, 0] = load_weight("w1_raw10", w1, 1, 0)
-        for q in range(4):
+        w1_raw[1, 0] = load_weight("w1_raw10", w1, 1, 0, RAW_AT[1])
+        w2_raw = load_w2(0)
+        tabs = [load_table(0)]
+        for q in range(QUADRANTS):
             nc.sync.dma_start(
                 out=w2_sc_raw[32 * q : 32 * q + 4, :, :].bitcast(I32),
-                in_=w2_scales[:, 4 * q : 4 * q + 4, :].rearrange("a r c -> r a c").bitcast(I32),
+                in_=w2_scales[:, 4 * q : 4 * q + 4, :].rearrange("g r c -> r g c").bitcast(I32),
             )
-        w2_raw = placed.tile([P, 2, 2 * H], U8, name="w2_raw", offset=W2_AT)
-        nc.sync.dma_start(out=w2_raw[:].bitcast(I32), in_=w2_words.rearrange("a p c -> p a c").bitcast(I32))
-        tabs = []
-        for a in range(2):
-            tab = placed.tile([P, T], U32, name=f"tab{a}", offset=TAB_AT[a])
+        tabs.append(load_table(1))
+
+        nc.vector.tensor_copy(v_planes[0][:], tab_sc[:].indirect(idx1[:]))
+        for q in range(QUADRANTS):
             nc.sync.dma_start(
-                out=tab[:].bitcast(I32), in_=tab_words[a].rearrange("p t i -> p (t i)").bitcast(I32)
+                out=v_planes[1][32 * q : 32 * q + 4, :].bitcast(I32),
+                in_=v_planes[0][32 * q + 4 : 32 * q + 8, :].bitcast(I32),
             )
-            tabs.append(tab)
-        for a in range(2):
-            nc.vector.tensor_copy(v_planes[a][:], tab_sc[:, a, :].indirect(idx1[:]))
 
         w1_q = {}
-        w1_bf = [deal_weight(w1_raw[a, 0], nc.scalar.copy) for a in range(2)]
+        w1_bf = [deal_weight(w1_raw[g, 0], nc.scalar.copy, staging()) for g in range(2)]
 
-        w2_codes = held("w2_codes", [P, 2, 2 * H], U8)
-        w2_sc = held("w2_sc", [P, 2, H], U8)
-        nc.vector.tensor_copy(
-            w2_codes[:].bitcast(U16).rearrange("p a (b t m) -> p (a b) m t", b=2, t=PACK),
-            w2_raw[:].bitcast(U16).rearrange("p a (b m t) -> p (a b) m t", b=2, t=PACK),
-        )
-        nc.vector.tensor_copy(
-            w2_sc[:].rearrange("p a (b t m) -> p (a b) m t", b=2, t=PACK),
-            w2_sc_raw[:].rearrange("p a (b m t) -> p (a b) m t", b=2, t=PACK),
-        )
-        for a in range(2):
-            w1_raw[a, 1] = load_weight(f"w1_raw{a}1", w1, a, 1)
-        weights = placed.tile([P, 2, M], F32, name="weights", offset=W2_AT)
-        wgt_sb, wgo_sb = weights[:, 0, :], weights[:, 1, :]
-        gain_sb = ring.tile([P, 2, PACK], F32, name="gain_sb", tag="w2_sc_raw", bufs=1, align_bytes=64)
-        nc.sync.dma_start(out=wgt_sb, in_=wgt)
-        nc.sync.dma_start(out=gain_sb[:], in_=gain.rearrange("(b p i) -> p b i", b=2, i=PACK))
-        nc.sync.dma_start(out=wgo_sb, in_=wgo)
-        w3_raw = {}
-        for a in range(2):
-            w1_q[a, 0] = quantise(f"w1_{a}0", w1_bf[a])
+        w2_codes = [held(f"w2_codes{b}", [P, 2, BANK], U16) for b in range(2)]
+        w2_sc = [held(f"w2_sc{b}", [P, 2, BANK], U8) for b in range(2)]
+
+        def deal_w2_words(b, raw):
+            nc.vector.tensor_copy(
+                w2_codes[b][:].rearrange("p g (i m) -> p g i m", i=PACK),
+                raw[:].bitcast(U16).rearrange("p g (m i) -> p g i m", i=PACK),
+            )
+
+        def deal_w2_scales(b):
+            nc.vector.tensor_copy(
+                w2_sc[b][:].rearrange("p g (i m) -> p g i m", i=PACK),
+                w2_sc_raw[:, :, BANK * b : BANK * (b + 1)].rearrange("p g (m i) -> p g i m", i=PACK),
+            )
 
         v_words = {}
 
-        def gather_words(a, u):
-            words = held(f"v_words{a}{u}", [P, BANK], U32)
-            cols = BANK // 16
-            nc.vector.tensor_copy(words[:], tabs[a][:].indirect(idx1[:, cols * u : cols * (u + 1)]))
-            v_words[a, u] = words
+        def gather_words(g, u):
+            words = held(f"v_words{g}{u}", [P, BANK], U32)
+            nc.vector.tensor_copy(words[:], tabs[g][:].indirect(entries(idx1, BANK * u, BANK)))
+            v_words[g, u] = words
 
-        for a in range(2):
-            for u in range(2):
-                gather_words(a, u)
+        deal_w2_words(0, w2_raw)
+        for g in range(2):
+            codes = placed.tile([P, BANK], U32, name=f"w1_{g}0_codes", offset=TAB_SC_AT + 4 * BANK * g, align_bytes=64)
+            w1_q[g, 0] = quantise(f"w1_{g}0", w1_bf[g], codes)
+        gather_words(0, 0)
+        deal_w2_scales(0)
+        gather_words(0, 1)
+        gather_words(1, 0)
+        gather_words(1, 1)
 
-        def product_a(acc, a, b, t, u):
-            codes, scales = w1_q[a, b]
-            cols = slice(P * t, P * (t + 1))
+        for g in range(2):
+            w1_raw[g, 1] = load_weight(f"w1_raw{g}1", w1, g, BANK, RAW_AT[g])
+        w2_raw = load_w2(1)
+        weights = placed.tile([P, 2, M], F32, name="weights", offset=WEIGHTS_AT)
+        wgt_sb, wgo_sb = weights[:, 0, :], weights[:, 1, :]
+        gain_sb = placed.tile([P, 2, PACK], F32, name="gain_sb", offset=GAIN_AT)
+        nc.sync.dma_start(out=wgt_sb, in_=wgt)
+        nc.sync.dma_start(out=gain_sb[:], in_=gain.rearrange("(b p i) -> p b i", b=2, i=PACK))
+        nc.sync.dma_start(out=wgo_sb, in_=wgo)
+        w3_raw = [load_weight(f"w3_raw{b}", w3, b, 0, W3_AT + RAW_BYTES * b) for b in range(2)]
+
+        def first_product(acc, lhsT, lhsT_scale, g, u):
             nc.tensor.matmul_mx(
                 out=acc[:],
-                lhsT=codes[:, cols].bitcast(FP8X4),
-                lhsT_scale=scales[:, cols],
-                rhs=v_words[a, u][:].bitcast(FP8X4),
-                rhs_scale=v_planes[a][:, BANK * u : BANK * (u + 1)],
-                start=(a == 0),
-                stop=(a == 1),
+                lhsT=lhsT,
+                lhsT_scale=lhsT_scale,
+                rhs=v_words[g, u][:].bitcast(FP8X4),
+                rhs_scale=v_planes[g][:, BANK * u : BANK * (u + 1)],
+                start=(g == 0),
+                stop=(g == 1),
             )
 
-        def product_b(acc, a, b, t, u):
-            first = BANK * b + P * t
-            nc.tensor.matmul_mx(
-                out=acc[:],
-                lhsT=w2_codes[:, a, 2 * first : 2 * (first + P)].bitcast(FP4X4),
-                lhsT_scale=w2_sc[:, a, first : first + P],
-                rhs=v_words[a, u][:].bitcast(FP8X4),
-                rhs_scale=v_planes[a][:, BANK * u : BANK * (u + 1)],
-                start=(a == 0),
-                stop=(a == 1),
-            )
+        def product_a(acc, g, b, u, i):
+            codes, scales = w1_q[g, b]
+            cols = slice(P * i, P * (i + 1))
+            first_product(acc, codes[:, cols].bitcast(FP8X4), scales[:, cols], g, u)
 
-        logs = [held(f"log{s}", [P, S], F32) for s in range(2 * PACK)]
-        rows = [held(f"row{s}", [P, S], F32) for s in range(2 * PACK)]
+        def product_b(acc, g, b, u, i):
+            cols = slice(P * i, P * (i + 1))
+            first_product(acc, w2_codes[b][:, g, cols].bitcast(FP4X4), w2_sc[b][:, g, cols], g, u)
 
-        def leave_psum(acc_a, acc_b, b, t, u):
-            s = PACK * b + t
-            cols = slice(BANK * u, BANK * (u + 1))
-            sq = ring.tile([P, BANK], F32, name="sq", tag="sq", bufs=4)
-            nc.scalar.activation(sq[:], acc_a[:], ACT.Square)
-            nc.vector.tensor_tensor(rows[s][:, cols], acc_b[:], sq[:], ADD)
-            nc.scalar.activation(logs[s][:, cols], sq[:], ACT.Ln, bias=act_const[:])
+        logs = [held(f"log{s}", [P, S], F32) for s in range(ROW_TILES)]
+        rows = [held(f"row{s}", [P, S], F32) for s in range(ROW_TILES)]
+        steps = [(b, u, i) for b in range(2) for u in range(2) for i in range(PACK)]
+        last_sq = [held(f"last_sq{b}", [P, 2 * BANK], F32) for b in range(2)]
+        first_of_last = len(steps) - 4
 
-        w3_q = {}
-        for b in range(2):
-            for u in range(2):
-                accs = [
-                    (psum.tile([P, BANK], F32, name="acc_a", tag="acc_a"), psum.tile([P, BANK], F32, name="acc_b", tag="acc_b"))
-                    for t in range(PACK)
-                ]
-                first_group = b == 0 and u == 0
-                if first_group:
-                    for t in range(PACK):
-                        product_a(accs[t][0], 0, b, t, u)
-                        product_b(accs[t][1], 0, b, t, u)
-                for t in range(PACK):
-                    for product, acc in zip((product_a, product_b), accs[t]):
-                        for a in range(1 if first_group else 0, 2):
-                            product(acc, a, b, t, u)
-                    leave_psum(accs[t][0], accs[t][1], b, t, u)
-                    if b == 0 and u == 0 and t in (1, 3):
-                        a = t // 2
-                        w1_bf[a] = deal_weight(w1_raw[a, 1], nc.vector.tensor_copy)
-                        w3_raw[a] = load_weight(f"w3_raw{a}", w3, a, 0)
-                    if b == 0 and (u, t) in ((0, 2), (1, 0)):
-                        a = u
-                        w1_q[a, 1] = quantise(f"w1_{a}1", w1_bf[a])
-                    if b == 1 and t == 0:
-                        w1_bf[u] = deal_weight(w3_raw[u], nc.vector.tensor_copy)
-                    if b == 1 and t == 1:
-                        w3_q[u] = quantise(f"w3_{u}", w1_bf[u])
+        def take_log(sq, b, u, i):
+            nc.scalar.activation(logs[PACK * b + i][:, BANK * u : BANK * (u + 1)], sq, ACT.Ln, bias=act_const[:])
 
-        nc.scalar.copy(act_const[:], neg_half[:])
-        picked = [
-            placed.tile([P, 2, PACK, HALF], F32, name=f"picked{b}", offset=TAB_AT[b]) for b in range(2)
+        def deal_w1_later(g):
+            w1_bf[g] = deal_weight(w1_raw[g, 1], nc.vector.tensor_copy, staging())
+
+        def quantise_w1_later(g):
+            w1_q[g, 1] = quantise_held(f"w1_{g}1", w1_bf[g])
+
+        later_operands = [
+            lambda: deal_w2_scales(1),
+            lambda: deal_w2_words(1, w2_raw),
+            lambda: deal_w1_later(0),
+            lambda: quantise_w1_later(0),
+            lambda: deal_w1_later(1),
+            lambda: quantise_w1_later(1),
         ]
 
-        def finish_row(s):
-            nc.scalar.activation(logs[s][:], logs[s][:], ACT.Sigmoid, scale=act_const[:])
-            nc.vector.tensor_tensor(rows[s][:], rows[s][:], logs[s][:], MULT)
+        accs = {}
+        pending_log = None
+        for n, (b, u, i) in enumerate(steps):
+            if n % IN_PSUM == 0:
+                for ahead in range(n, n + IN_PSUM):
+                    accs[ahead] = (
+                        psum.tile([P, BANK], F32, name="acc_a", tag="acc_a"),
+                        psum.tile([P, BANK], F32, name="acc_b", tag="acc_b"),
+                    )
+                    if n == 0:
+                        product_a(accs[ahead][0], 0, *steps[ahead])
+                        product_b(accs[ahead][1], 0, *steps[ahead])
+            acc_a, acc_b = accs[n]
+            for product, acc in ((product_a, acc_a), (product_b, acc_b)):
+                for g in range(1 if n < IN_PSUM else 0, 2):
+                    product(acc, g, b, u, i)
+            if n < first_of_last:
+                sq_tile = ring.tile([P, BANK], F32, name="sq", tag="sq", bufs=IN_PSUM)
+                sq = sq_tile[:]
+            else:
+                tile_no, side = divmod(n - first_of_last, 2)
+                sq = last_sq[tile_no][:, BANK * side : BANK * (side + 1)]
+            nc.scalar.activation(sq, acc_a[:], ACT.Square)
+            if pending_log is not None:
+                take_log(*pending_log)
+            pending_log = (sq, b, u, i)
+            nc.vector.tensor_tensor(rows[PACK * b + i][:, BANK * u : BANK * (u + 1)], acc_b[:], sq, ADD)
+            if n < len(later_operands):
+                later_operands[n]()
+        take_log(*pending_log)
+        w3_bf = [deal_weight(w3_raw[b], nc.vector.tensor_copy, last_sq[b][:].bitcast(BF16)) for b in range(2)]
+        w3_q = [quantise_held(f"w3_{b}", w3_bf[b]) for b in range(2)]
+
+        nc.scalar.copy(act_const[:], neg_half[:])
+        first_picks = placed.tile([P, 2, PACK * HALF], F32, name="first_picks", offset=PICKS_AT)
+        picked = [[first_picks[:, b, :], logs[ROW_TILES - 2 + b][:]] for b in range(2)]
+
+        def finish_row(s, cols=slice(0, S)):
+            nc.scalar.activation(logs[s][:, cols], logs[s][:, cols], ACT.Sigmoid, scale=act_const[:])
+            nc.vector.tensor_tensor(rows[s][:, cols], rows[s][:, cols], logs[s][:, cols], MULT)
+
+        def picked_of(s, half):
+            b, i = divmod(s, PACK)
+            return picked[b][half][:, HALF * i : HALF * (i + 1)]
 
         def pick(s, half):
-            b, i = divmod(s, PACK)
-            cols = HALF // 16
-            x = picked[b][:, half, i, :]
+            x = picked_of(s, half)
             nc.vector.tensor_tensor(
                 x,
-                rows[s][:].indirect(idx2[:, cols * half : cols * (half + 1)]),
+                rows[s][:].indirect(entries(idx2, HALF * half, HALF)),
                 wgt_sb[:, HALF * half : HALF * (half + 1)],
                 MULT,
             )
             nc.scalar.activation(x, x, ACT.Tanh)
+
+        z_bf = {}
+
+        def finish_pick(s, half):
+            b, i = divmod(s, PACK)
+            x = picked_of(s, half)
             nc.scalar.activation(x, x, ACT.Copy, scale=gain_sb[:, b, i : i + 1])
-
-        def weave(b, half):
-            z_bf = ring.tile([P, PACK * HALF], BF16, name="z_bf", tag="z_bf", bufs=2, align_bytes=64)
-            nc.scalar.copy(
-                z_bf[:].rearrange("p (c n i) -> p c i n", n=4, i=PACK),
-                picked[b][:, half, :, :].rearrange("p i (c n) -> p c i n", n=4),
-            )
-            return z_bf
-
-        def product_y(accs, b, z_q):
-            codes, scales = w3_q[b]
-            for i in range(PACK):
-                cols = slice(P * i, P * (i + 1))
-                nc.tensor.matmul_mx(
-                    out=accs[i][:],
-                    lhsT=codes[:, cols].bitcast(FP8X4),
-                    lhsT_scale=scales[:, cols],
-                    rhs=z_q[0][:].bitcast(FP8X4),
-                    rhs_scale=z_q[1][:],
-                    start=(b == 0),
-                    stop=(b == 1),
+            if i == PACK - 1:
+                woven = held(f"z_bf{b}{half}", [P, PACK * HALF], BF16)
+                nc.scalar.copy(
+                    woven[:].rearrange("p (c n j) -> p c j n", n=4, j=PACK),
+                    picked[b][half].rearrange("p (j c n) -> p c j n", j=PACK, n=4),
                 )
-
-        def place(accs, half):
-            cols = HALF // 16
-            for i in range(PACK):
-                y = ring.tile([P, HALF], F32, name="y", tag="y", bufs=4)
-                nc.scalar.copy(y[:], accs[i][:])
-                nc.vector.tensor_tensor(
-                    pages[i][:].indirect(idx3[:, cols * half : cols * (half + 1)]),
-                    y[:],
-                    wgo_sb[:, HALF * half : HALF * (half + 1)],
-                    MULT,
-                )
-                if half == 1:
-                    nc.sync.dma_start(out=out.rearrange("(p i) c -> i p c", i=PACK)[i], in_=pages[i][:])
+                z_bf[b, half] = woven[:]
 
         y_accs = [
             [psum.tile([P, HALF], F32, name="acc_y", tag=tag) for i in range(PACK)] for tag in ("acc_a", "acc_b")
         ]
-        z_bf = {}
-        finish_row(0)
-        for s in range(2 * PACK):
-            if s + 1 < 2 * PACK:
+
+        def product_y(b, half):
+            z_codes, z_scales = quantise_held(f"z{b}{half}", z_bf[b, half])
+            codes, scales = w3_q[b]
+            for i in range(PACK):
+                cols = slice(P * i, P * (i + 1))
+                nc.tensor.matmul_mx(
+                    out=y_accs[half][i][:],
+                    lhsT=codes[:, cols].bitcast(FP8X4),
+                    lhsT_scale=scales[:, cols],
+                    rhs=z_codes[:].bitcast(FP8X4),
+                    rhs_scale=z_scales[:],
+                    start=(b == 0),
+                    stop=(b == 1),
+                )
+
+        def y_staging():
+            y_tile = ring.tile([P, HALF], F32, name="y", tag="y", bufs=PACK)
+            return y_tile[:]
+
+        def place(i, half, y):
+            nc.scalar.copy(y, y_accs[half][i][:])
+            nc.vector.tensor_tensor(
+                pages[i][:].indirect(entries(idx3, HALF * half, HALF)),
+                y,
+                wgo_sb[:, HALF * half : HALF * (half + 1)],
+                MULT,
+            )
+
+        finish_row(0, slice(0, S // 2))
+        finish_row(0, slice(S // 2, S))
+        for s in range(ROW_TILES):
+            if s + 1 < ROW_TILES:
                 finish_row(s + 1)
             pick(s, 0)
-            if s % PACK == PACK - 1:
-                z_bf[s // PACK, 0] = weave(s // PACK, 0)
-            if s == PACK + 1:
-                product_y(y_accs[0], 0, quantise("z00", z_bf[0, 0]))
-        for s in range(2 * PACK):
+            if s > 0:
+                finish_pick(s - 1, 0)
+            if s == PACK + 2:
+                product_y(0, 0)
+        for s in range(ROW_TILES):
             pick(s, 1)
-            if s % PACK == PACK - 1:
-                z_bf[s // PACK, 1] = weave(s // PACK, 1)
+            if s == 0:
+                finish_pick(ROW_TILES - 1, 0)
+            else:
+                finish_pick(s - 1, 1)
             if s == PACK:
-                product_y(y_accs[0], 1, quantise("z10", z_bf[1, 0]))
-        product_y(y_accs[1], 0, quantise("z01", z_bf[0, 1]))
-        place(y_accs[0], 0)
-        product_y(y_accs[1], 1, quantise("z11", z_bf[1, 1]))
-        place(y_accs[1], 1)
+                product_y(1, 0)
+        finish_pick(ROW_TILES - 1, 1)
+        product_y(0, 1)
+        for i in range(PACK - 1):
+            place(i, 0, y_staging())
+        product_y(1, 1)
+        place(PACK - 1, 0, z_bf[1, 1].bitcast(F32)[:, :HALF])
+        out_rows = out.rearrange("(p i) c -> i p c", i=PACK)
+        for i in range(PACK):
+            place(i, 1, y_staging())
+            nc.sync.dma_start(out=out_rows[i], in_=pages[i][:])

from contextlib import ExitStack

import concourse.mybir as mybir

F32 = mybir.dt.float32
BF16 = mybir.dt.bfloat16
I32 = mybir.dt.int32
U32 = mybir.dt.uint32
U16 = mybir.dt.uint16
U8 = mybir.dt.uint8
FP8X4 = mybir.dt.float8_e4m3fn_x4
FP4X4 = mybir.dt.float4_e2m1fn_x4
ACT = mybir.ActivationFunctionType
ADD = mybir.AluOpType.add
MULT = mybir.AluOpType.mult

T, S, M, T2, K, H, N = 4096, 1024, 512, 1024, 1024, 1024, 512
FLOPS = 2 * (2 * K * H * S + H * N * M)

P = 128
PACK = 4
PASS = P * PACK
BANK = 512
QUADRANTS = 4
PER_COLUMN = 16
ROW_TILES = H // P
HALF = M // 2
IN_PSUM = 4
LN_FLOOR = 2.0**-60

RAW_BYTES = PACK * BANK * 4
RAW_AT = (0, RAW_BYTES)
W2_AT = 2 * RAW_BYTES
TAB_AT = (W2_AT + 2 * H, W2_AT + 2 * H + 4 * T)
TAB_SC_AT = TAB_AT[1] + 4 * T
PICKS_AT = TAB_AT[0]
WEIGHTS_AT = PICKS_AT + ROW_TILES * HALF * 4
GAIN_AT = WEIGHTS_AT + 2 * M * 4
W3_AT = TAB_AT[1]


def tile_list_muon_void_scores_kernel(
    tc, tab_words, tab_scales, offs, offs2, offs3, w1, w2_words, w2_scales, w3, gain, wgt, wgo, out
):
    nc = tc.nc
    with ExitStack() as ctx:
        lists = ctx.enter_context(tc.tile_pool(name="lists", bufs=1))
        keep = ctx.enter_context(tc.tile_pool(name="keep", bufs=1))
        ring = ctx.enter_context(tc.tile_pool(name="ring", bufs=1))
        placed = ctx.enter_context(tc.tile_pool(name="placed", bufs=1))
        psum = ctx.enter_context(tc.psum_pool(name="psum", bufs=IN_PSUM))

        def held(name, shape, dtype):
            return keep.tile(shape, dtype, name=name, align_bytes=64)

        def entries(idx, first, count):
            return idx[:, first // PER_COLUMN : (first + count) // PER_COLUMN]

        idx1 = lists.tile([P, S // PER_COLUMN], U16, name="idx1")
        idx2 = lists.tile([P, M // PER_COLUMN], U16, name="idx2")
        idx3 = lists.tile([P, M // PER_COLUMN], U16, name="idx3")

        tab_sc = placed.tile([P, T], U8, name="tab_sc", offset=TAB_SC_AT)
        w2_sc_raw = held("w2_sc_raw", [P, 2, H], U8)
        v_planes = [held(f"v_plane{g}", [P, S], U8) for g in range(2)]
        act_const = held("act_const", [P, 1], F32)
        neg_half = held("neg_half", [P, 1], F32)
        warm = held("warm", [P, 1], F32)
        pages = [held(f"page{i}", [P, T2], F32) for i in range(PACK)]

        nc.vector.memset(tab_sc[:].bitcast(I32), 0)
        nc.vector.memset(act_const[:], LN_FLOOR)
        nc.vector.memset(neg_half[:], -0.5)
        nc.vector.memset(w2_sc_raw[:].rearrange("p g c -> p (g c)").bitcast(I32), 0)
        nc.vector.memset(v_planes[1][:].bitcast(I32), 0)
        nc.scalar.activation(warm[:], act_const[:], ACT.Ln)
        for page in pages:
            nc.vector.memset(page[:], 0.0)

        def load_weight(name, w, g, first_column, at):
            raw = placed.tile([P, PACK, BANK], F32, name=name, offset=at)
            nc.sync.dma_start(
                out=raw[:],
                in_=w[PASS * g : PASS * (g + 1), first_column : first_column + BANK].rearrange(
                    "(p j) c -> p j c", j=PACK
                ),
            )
            return raw

        def load_w2(b):
            raw = placed.tile([P, 2, 2 * BANK], U8, name=f"w2_raw{b}", offset=W2_AT)
            nc.sync.dma_start(
                out=raw[:].bitcast(I32),
                in_=w2_words[:, :, 2 * BANK * b : 2 * BANK * (b + 1)].rearrange("g p c -> p g c").bitcast(I32),
            )
            return raw

        def load_table(g):
            tab = placed.tile([P, T], U32, name=f"tab{g}", offset=TAB_AT[g])
            nc.sync.dma_start(out=tab[:].bitcast(I32), in_=tab_words[g].rearrange("p t i -> p (t i)").bitcast(I32))
            return tab

        def staging():
            staged = ring.tile([P, PACK * BANK], BF16, name="w_bf", tag="w_bf", bufs=2, align_bytes=64)
            return staged[:]

        def deal_weight(raw, copy, staged):
            copy(
                staged.rearrange("p (i m j) -> p m j i", i=PACK, j=PACK),
                raw[:].rearrange("p j (m i) -> p m j i", i=PACK),
            )
            return staged

        def quantise(name, staged, codes):
            scales = held(name + "_scales", [P, codes.shape[1]], U8)
            nc.vector.quantize_mx(out=codes[:].bitcast(FP8X4), scales=scales[:], in_=staged)
            return codes, scales

        def quantise_held(name, staged):
            return quantise(name, staged, held(name + "_codes", [P, staged.shape[1] // PACK], U32))

        nc.sync.dma_start(idx1[:], offs)
        nc.sync.dma_start(idx2[:], offs2)
        nc.sync.dma_start(idx3[:], offs3)
        w1_raw = {(0, 0): load_weight("w1_raw00", w1, 0, 0, RAW_AT[0])}
        for q in range(QUADRANTS):
            nc.sync.dma_start(
                out=tab_sc[32 * q : 32 * q + 8, :].bitcast(I32),
                in_=tab_scales[:, 4 * q : 4 * q + 4, :].bitcast(I32),
            )
        w1_raw[1, 0] = load_weight("w1_raw10", w1, 1, 0, RAW_AT[1])
        w2_raw = load_w2(0)
        tabs = [load_table(0)]
        for q in range(QUADRANTS):
            nc.sync.dma_start(
                out=w2_sc_raw[32 * q : 32 * q + 4, :, :].bitcast(I32),
                in_=w2_scales[:, 4 * q : 4 * q + 4, :].rearrange("g r c -> r g c").bitcast(I32),
            )
        tabs.append(load_table(1))

        nc.vector.tensor_copy(v_planes[0][:], tab_sc[:].indirect(idx1[:]))
        for q in range(QUADRANTS):
            nc.sync.dma_start(
                out=v_planes[1][32 * q : 32 * q + 4, :].bitcast(I32),
                in_=v_planes[0][32 * q + 4 : 32 * q + 8, :].bitcast(I32),
            )

        w1_q = {}
        w1_bf = [deal_weight(w1_raw[g, 0], nc.scalar.copy, staging()) for g in range(2)]

        w2_codes = [held(f"w2_codes{b}", [P, 2, BANK], U16) for b in range(2)]
        w2_sc = [held(f"w2_sc{b}", [P, 2, BANK], U8) for b in range(2)]

        def deal_w2_words(b, raw):
            nc.vector.tensor_copy(
                w2_codes[b][:].rearrange("p g (i m) -> p g i m", i=PACK),
                raw[:].bitcast(U16).rearrange("p g (m i) -> p g i m", i=PACK),
            )

        def deal_w2_scales(b):
            nc.vector.tensor_copy(
                w2_sc[b][:].rearrange("p g (i m) -> p g i m", i=PACK),
                w2_sc_raw[:, :, BANK * b : BANK * (b + 1)].rearrange("p g (m i) -> p g i m", i=PACK),
            )

        v_words = {}

        def gather_words(g, u):
            words = held(f"v_words{g}{u}", [P, BANK], U32)
            nc.vector.tensor_copy(words[:], tabs[g][:].indirect(entries(idx1, BANK * u, BANK)))
            v_words[g, u] = words

        deal_w2_words(0, w2_raw)
        for g in range(2):
            codes = placed.tile([P, BANK], U32, name=f"w1_{g}0_codes", offset=TAB_SC_AT + 4 * BANK * g, align_bytes=64)
            w1_q[g, 0] = quantise(f"w1_{g}0", w1_bf[g], codes)
        gather_words(0, 0)
        deal_w2_scales(0)
        gather_words(0, 1)
        gather_words(1, 0)
        gather_words(1, 1)

        for g in range(2):
            w1_raw[g, 1] = load_weight(f"w1_raw{g}1", w1, g, BANK, RAW_AT[g])
        w2_raw = load_w2(1)
        weights = placed.tile([P, 2, M], F32, name="weights", offset=WEIGHTS_AT)
        wgt_sb, wgo_sb = weights[:, 0, :], weights[:, 1, :]
        gain_sb = placed.tile([P, 2, PACK], F32, name="gain_sb", offset=GAIN_AT)
        nc.sync.dma_start(out=wgt_sb, in_=wgt)
        nc.sync.dma_start(out=gain_sb[:], in_=gain.rearrange("(b p i) -> p b i", b=2, i=PACK))
        nc.sync.dma_start(out=wgo_sb, in_=wgo)
        w3_raw = [load_weight(f"w3_raw{b}", w3, b, 0, W3_AT + RAW_BYTES * b) for b in range(2)]

        def first_product(acc, lhsT, lhsT_scale, g, u):
            nc.tensor.matmul_mx(
                out=acc[:],
                lhsT=lhsT,
                lhsT_scale=lhsT_scale,
                rhs=v_words[g, u][:].bitcast(FP8X4),
                rhs_scale=v_planes[g][:, BANK * u : BANK * (u + 1)],
                start=(g == 0),
                stop=(g == 1),
            )

        def product_a(acc, g, b, u, i):
            codes, scales = w1_q[g, b]
            cols = slice(P * i, P * (i + 1))
            first_product(acc, codes[:, cols].bitcast(FP8X4), scales[:, cols], g, u)

        def product_b(acc, g, b, u, i):
            cols = slice(P * i, P * (i + 1))
            first_product(acc, w2_codes[b][:, g, cols].bitcast(FP4X4), w2_sc[b][:, g, cols], g, u)

        logs = [held(f"log{s}", [P, S], F32) for s in range(ROW_TILES)]
        rows = [held(f"row{s}", [P, S], F32) for s in range(ROW_TILES)]
        steps = [(b, u, i) for b in range(2) for u in range(2) for i in range(PACK)]
        last_sq = [held(f"last_sq{b}", [P, 2 * BANK], F32) for b in range(2)]
        first_of_last = len(steps) - 4

        def take_log(sq, b, u, i):
            nc.scalar.activation(logs[PACK * b + i][:, BANK * u : BANK * (u + 1)], sq, ACT.Ln, bias=act_const[:])

        def deal_w1_later(g):
            w1_bf[g] = deal_weight(w1_raw[g, 1], nc.vector.tensor_copy, staging())

        def quantise_w1_later(g):
            w1_q[g, 1] = quantise_held(f"w1_{g}1", w1_bf[g])

        later_operands = [
            lambda: deal_w2_scales(1),
            lambda: deal_w2_words(1, w2_raw),
            lambda: deal_w1_later(0),
            lambda: quantise_w1_later(0),
            lambda: deal_w1_later(1),
            lambda: quantise_w1_later(1),
        ]

        accs = {}
        pending_log = None
        for n, (b, u, i) in enumerate(steps):
            if n % IN_PSUM == 0:
                for ahead in range(n, n + IN_PSUM):
                    accs[ahead] = (
                        psum.tile([P, BANK], F32, name="acc_a", tag="acc_a"),
                        psum.tile([P, BANK], F32, name="acc_b", tag="acc_b"),
                    )
                    if n == 0:
                        product_a(accs[ahead][0], 0, *steps[ahead])
                        product_b(accs[ahead][1], 0, *steps[ahead])
            acc_a, acc_b = accs[n]
            for product, acc in ((product_a, acc_a), (product_b, acc_b)):
                for g in range(1 if n < IN_PSUM else 0, 2):
                    product(acc, g, b, u, i)
            if n < first_of_last:
                sq_tile = ring.tile([P, BANK], F32, name="sq", tag="sq", bufs=IN_PSUM)
                sq = sq_tile[:]
            else:
                tile_no, side = divmod(n - first_of_last, 2)
                sq = last_sq[tile_no][:, BANK * side : BANK * (side + 1)]
            nc.scalar.activation(sq, acc_a[:], ACT.Square)
            if pending_log is not None:
                take_log(*pending_log)
            pending_log = (sq, b, u, i)
            nc.vector.tensor_tensor(rows[PACK * b + i][:, BANK * u : BANK * (u + 1)], acc_b[:], sq, ADD)
            if n < len(later_operands):
                later_operands[n]()
        take_log(*pending_log)
        w3_bf = [deal_weight(w3_raw[b], nc.vector.tensor_copy, last_sq[b][:].bitcast(BF16)) for b in range(2)]
        w3_q = [quantise_held(f"w3_{b}", w3_bf[b]) for b in range(2)]

        nc.scalar.copy(act_const[:], neg_half[:])
        first_picks = placed.tile([P, 2, PACK * HALF], F32, name="first_picks", offset=PICKS_AT)
        picked = [[first_picks[:, b, :], logs[ROW_TILES - 2 + b][:]] for b in range(2)]

        def finish_row(s, cols=slice(0, S)):
            nc.scalar.activation(logs[s][:, cols], logs[s][:, cols], ACT.Sigmoid, scale=act_const[:])
            nc.vector.tensor_tensor(rows[s][:, cols], rows[s][:, cols], logs[s][:, cols], MULT)

        def picked_of(s, half):
            b, i = divmod(s, PACK)
            return picked[b][half][:, HALF * i : HALF * (i + 1)]

        def pick(s, half):
            x = picked_of(s, half)
            nc.vector.tensor_tensor(
                x,
                rows[s][:].indirect(entries(idx2, HALF * half, HALF)),
                wgt_sb[:, HALF * half : HALF * (half + 1)],
                MULT,
            )
            nc.scalar.activation(x, x, ACT.Tanh)

        z_bf = {}

        def finish_pick(s, half):
            b, i = divmod(s, PACK)
            x = picked_of(s, half)
            nc.scalar.activation(x, x, ACT.Copy, scale=gain_sb[:, b, i : i + 1])
            if i == PACK - 1:
                woven = held(f"z_bf{b}{half}", [P, PACK * HALF], BF16)
                nc.scalar.copy(
                    woven[:].rearrange("p (c n j) -> p c j n", n=4, j=PACK),
                    picked[b][half].rearrange("p (j c n) -> p c j n", j=PACK, n=4),
                )
                z_bf[b, half] = woven[:]

        y_accs = [
            [psum.tile([P, HALF], F32, name="acc_y", tag=tag) for i in range(PACK)] for tag in ("acc_a", "acc_b")
        ]

        def product_y(b, half):
            z_codes, z_scales = quantise_held(f"z{b}{half}", z_bf[b, half])
            codes, scales = w3_q[b]
            for i in range(PACK):
                cols = slice(P * i, P * (i + 1))
                nc.tensor.matmul_mx(
                    out=y_accs[half][i][:],
                    lhsT=codes[:, cols].bitcast(FP8X4),
                    lhsT_scale=scales[:, cols],
                    rhs=z_codes[:].bitcast(FP8X4),
                    rhs_scale=z_scales[:],
                    start=(b == 0),
                    stop=(b == 1),
                )

        def y_staging():
            y_tile = ring.tile([P, HALF], F32, name="y", tag="y", bufs=PACK)
            return y_tile[:]

        def place(i, half, y):
            nc.scalar.copy(y, y_accs[half][i][:])
            nc.vector.tensor_tensor(
                pages[i][:].indirect(entries(idx3, HALF * half, HALF)),
                y,
                wgo_sb[:, HALF * half : HALF * (half + 1)],
                MULT,
            )

        finish_row(0, slice(0, S // 2))
        finish_row(0, slice(S // 2, S))
        for s in range(ROW_TILES):
            if s + 1 < ROW_TILES:
                finish_row(s + 1)
            pick(s, 0)
            if s > 0:
                finish_pick(s - 1, 0)
            if s == PACK + 2:
                product_y(0, 0)
        for s in range(ROW_TILES):
            pick(s, 1)
            if s == 0:
                finish_pick(ROW_TILES - 1, 0)
            else:
                finish_pick(s - 1, 1)
            if s == PACK:
                product_y(1, 0)
        finish_pick(ROW_TILES - 1, 1)
        product_y(0, 1)
        for i in range(PACK - 1):
            place(i, 0, y_staging())
        product_y(1, 1)
        place(PACK - 1, 0, z_bf[1, 1].bitcast(F32)[:, :HALF])
        out_rows = out.rearrange("(p i) c -> i p c", i=PACK)
        for i in range(PACK):
            place(i, 1, y_staging())
            nc.sync.dma_start(out=out_rows[i], in_=pages[i][:])
